import numpy as np
import ml_dtypes


def mxq(x, axis, fmt="e4m3"):
    dtype, down = {"e4m3": (ml_dtypes.float8_e4m3fn, 7), "e5m2": (ml_dtypes.float8_e5m2, 14)}[fmt]
    v = np.moveaxis(np.asarray(x, np.float32).astype(ml_dtypes.bfloat16).astype(np.float64), axis, -1)
    blocks = v.reshape(v.shape[:-1] + (-1, 32))
    amax = np.abs(blocks).max(-1, keepdims=True)
    byte = np.maximum(np.where(amax > 0, np.frexp(amax)[1] - 1 + 127, 0) - down, 1)
    scale = np.exp2(byte - 127.0)
    codes = (blocks / scale).astype(np.float32).astype(dtype).astype(np.float64)
    return np.moveaxis((codes * scale).reshape(v.shape), -1, axis)


WIDE = False


def mx_kscale(k):
    if not WIDE:
        return np.ones(k)
    levels = np.array([10, -10, 5, -5, 0])
    if k % 512:
        return np.exp2(np.random.permutation(np.resize(levels, k // 32))).repeat(32)
    a = np.empty((k // 512, 16))
    for p in range(k // 512):
        a[p, :8] = np.random.permutation(np.resize(levels, 8))
        for g in range(8):
            far = levels[np.abs(levels - a[p, g]) >= 10]
            a[p, g + 8] = far[np.random.randint(len(far))]
    return np.exp2(a.ravel()).repeat(32)


def f64(x):
    return np.asarray(x).astype(np.float64)


def striped(idx):
    return np.tile(idx.reshape(-1, 16).T, (8, 1)).astype(np.uint16)


def unstriped(offs):
    return offs[:16].T.reshape(-1).astype(np.int64)


E2M1 = np.array([0.0, 0.5, 1.0, 1.5, 2.0, 3.0, 4.0, 6.0, -0.0, -0.5, -1.0, -1.5, -2.0, -3.0, -4.0, -6.0])


def pack_weight(w, fmt):
    k, n = w.shape
    w = f64(np.asarray(w, np.float32).astype(ml_dtypes.bfloat16)).reshape(k // 32, 32, n)
    amax = np.abs(w).max(1)
    if fmt == "e4m3":
        byte = np.frexp(amax)[1] - 1 + 127 - 7
    else:
        mant, ex = np.frexp(amax / 6.0)
        byte = np.where(mant > 0.5, ex, ex - 1) + 127
    byte = np.clip(np.where(amax > 0, byte, 1), 1, 254)
    scaled = (w * np.exp2(127.0 - byte)[:, None, :]).reshape(k, n).astype(np.float32)
    by_word = np.ascontiguousarray(scaled.reshape(k // 512, 128, 4, n).transpose(0, 1, 3, 2))
    if fmt == "e4m3":
        words = by_word.astype(ml_dtypes.float8_e4m3fn).view(np.uint8)
    else:
        c = by_word.astype(ml_dtypes.float4_e2m1fn).view(np.uint8) & 0xF
        words = (c[..., 0::2] | (c[..., 1::2] << 4)).reshape(k // 512, 128, 2 * n)
    return np.ascontiguousarray(words), np.ascontiguousarray(byte.astype(np.uint8).reshape(k // 512, 16, n))


def unpack_weight(words, scales, fmt):
    g, _, n = scales.shape
    words = np.ascontiguousarray(words).reshape(g, 128, n, -1)
    if fmt == "e4m3":
        vals = words.view(ml_dtypes.float8_e4m3fn).astype(np.float64)
    else:
        nib = np.empty((g, 128, n, 4), np.uint8)
        nib[..., 0::2] = words & 0xF
        nib[..., 1::2] = words >> 4
        vals = E2M1[nib]
    vals = vals * np.repeat(np.exp2(scales.astype(np.float64) - 127.0), 8, axis=1)[..., None]
    return vals.transpose(0, 1, 3, 2).reshape(g * 512, n)


K, T, E, C, N = 512, 640, 20, 128, 384
TOP = 4
M = 512


def by_expert(wq, xq):
    return np.concatenate([wq[e].T @ xq[:, e * C:(e + 1) * C] for e in range(E)], axis=1)


def setup_inputs():
    n = np.random.standard_normal
    s = mx_kscale(K)[:, None]
    deal = np.repeat(np.arange(E), C).reshape(TOP, T)[:, np.random.permutation(T)]
    deal = np.take_along_axis(deal, np.argsort(np.random.rand(TOP, T), axis=0), axis=0)
    for _ in range(8):
        s_, t_ = np.random.permutation(T).reshape(2, -1); r = np.random.randint(TOP, size=T // 2); x, y = deal[r, s_].copy(), deal[r, t_].copy()
        ok = ~((deal[:, s_] == y).any(0) | (deal[:, t_] == x).any(0)); deal[r[ok], s_[ok]] = y[ok]; deal[r[ok], t_[ok]] = x[ok]
    order = np.lexsort((np.random.rand(TOP * T), deal.reshape(-1)))
    slot_token = order % T; pos = np.empty(TOP * T, np.int64); pos[order] = np.arange(TOP * T); pos = pos.reshape(TOP, T)
    g = np.random.uniform(0.5, 1.5, (TOP, T)); g = g / g.sum(0)
    w = [pack_weight(m, "e2m1") for m in n((E, K, N)) / np.sqrt(K) / s[None]]
    r = mx_kscale(M)[:, None]
    return {
        "uT": (n((M, T)) * r).astype(np.float32),
        "wu": (n((M, K)) / np.sqrt(M) / r * s.T).astype(np.float32),
        "w_words": np.stack([m[0] for m in w]),
        "w_scales": np.stack([m[1] for m in w]),
        "gate": np.stack([np.tile(r, (N, 1)) for r in g]).astype(np.float32),
        "offs": striped(slot_token),
        "pos1": striped(pos[0]),
        "pos2": striped(pos[1]),
        "pos3": striped(pos[2]),
        "pos4": striped(pos[3]),
    }


def reference(uT, wu, w_words, w_scales, gate, offs, pos1, pos2, pos3, pos4):
    idx = unstriped(offs)
    w = np.stack([unpack_weight(w_words[e], w_scales[e], "e2m1") for e in range(E)])
    x = mxq(f64(wu), 0, "e4m3").T @ mxq(f64(uT), 0, "e4m3")
    xq = mxq(x[:, idx], 0, "e4m3")
    y = by_expert(w, xq)
    return sum(f64(gate[r]) * y[:, unstriped(p)] for r, p in enumerate((pos1, pos2, pos3, pos4)))

@@ -1,0 +1,238 @@
+from contextlib import ExitStack
+
+import concourse.mybir as mybir
+from concourse.masks import make_identity
+
+M, K, N, T = 512, 512, 384, 640
+E, C, TOP = 20, 128, 4
+S = E * C
+
+FLOPS = 2 * M * K * T + 2 * K * N * S
+
+F32 = mybir.dt.float32
+BF16 = mybir.dt.bfloat16
+I32 = mybir.dt.int32
+U32 = mybir.dt.uint32
+U16 = mybir.dt.uint16
+U8 = mybir.dt.uint8
+FP8X4 = mybir.dt.float8_e4m3fn_x4
+FP4X4 = mybir.dt.float4_e2m1fn_x4
+MULT = mybir.AluOpType.mult
+ADD = mybir.AluOpType.add
+
+P = 128
+PACK = 4
+BANK = 512
+PER_COL = 16
+WINDOW = 704
+TOKEN_CHUNKS = ((0, 256), (256, 256), (512, 128))
+SLOT_CHUNKS = ((0, 512), (512, 512), (1024, 512), (1536, 512), (2048, 256), (2304, 128), (2432, 128))
+EXPERTS_A_LOAD = 4
+WU_SPLIT = 88
+HALVES = ((0, 384), (384, 256))
+
+
+def tile_moe_prv_lin_none_kernel(tc, uT, wu, w_words, w_scales, gate, offs, pos1, pos2, pos3, pos4, out):
+    nc = tc.nc
+    with ExitStack() as ctx:
+        lists = ctx.enter_context(tc.tile_pool(name="lists", bufs=1))
+        keep = ctx.enter_context(tc.tile_pool(name="keep", bufs=1))
+        ring = ctx.enter_context(tc.tile_pool(name="ring", bufs=2))
+        prods = ctx.enter_context(tc.tile_pool(name="prods", bufs=6))
+        psum = ctx.enter_context(tc.psum_pool(name="psum", bufs=6))
+        late = ctx.enter_context(tc.psum_pool(name="late", bufs=2))
+
+        wu_rows = wu.rearrange("(p j) k -> p j k", j=PACK)
+        u_rows = uT.rearrange("(p j) t -> p j t", j=PACK)
+        wu_raw = keep.tile([P, PACK, K], F32, name="wu_raw")
+        nc.sync.dma_start(out=wu_raw[:], in_=wu_rows)
+        u_raw = []
+        for t0, width in TOKEN_CHUNKS:
+            raw = keep.tile([P, PACK, width], F32, name="u_raw%d" % t0)
+            nc.sync.dma_start(out=raw[:], in_=u_rows[:, :, t0:t0 + width])
+            u_raw.append(raw)
+        slot_tokens = lists.tile([P, S // PER_COL], U16, name="slot_tokens")
+        nc.sync.dma_start(slot_tokens[:], offs)
+
+        w_plane = keep.tile([P, E * N], U8, name="w_plane", align_bytes=64)
+        nc.vector.memset(w_plane[:].bitcast(I32), 0)
+        for r in range(4):
+            nc.sync.dma_start(
+                out=w_plane[r:P:32, :].bitcast(I32).rearrange("q (e n) -> q e n", e=E),
+                in_=w_scales[:, 0, r:16:4, :].bitcast(I32).rearrange("e q n -> q e n"),
+            )
+        w_codes = []
+        for g in range(E // EXPERTS_A_LOAD):
+            codes = keep.tile([P, EXPERTS_A_LOAD * 2 * N], U8, name="w_codes%d" % g, align_bytes=64)
+            nc.sync.dma_start(
+                out=codes[:].bitcast(I32).rearrange("p (e n) -> p e n", e=EXPERTS_A_LOAD),
+                in_=w_words[g * EXPERTS_A_LOAD:(g + 1) * EXPERTS_A_LOAD, 0, :, :].bitcast(I32).rearrange("e p n -> p e n"),
+            )
+            w_codes.append(codes)
+        token_slots = []
+        for r, pos in enumerate((pos1, pos2, pos3, pos4)):
+            one = lists.tile([P, T // PER_COL], U16, name="token_slots%d" % r)
+            nc.sync.dma_start(one[:], pos)
+            token_slots.append(one)
+        gates = keep.tile([P, TOP, T], F32, name="gates")
+        nc.sync.dma_start(out=gates[:], in_=gate[:, 0:P, :].rearrange("r p t -> p r t"))
+
+        ident = keep.tile([P, P], F32, name="ident")
+        make_identity(nc, ident[:])
+
+        x_pairs = []
+        for u in range(2):
+            pair = keep.tile([P, WINDOW], U32, name="x_pairs%d" % u)
+            nc.vector.memset(pair[:, T:WINDOW], 0)
+            x_pairs.append(pair)
+
+        wu_grouped = keep.tile([P, PACK, P, PACK], BF16, name="wu_grouped", align_bytes=64)
+        for copy, m0, m1 in ((nc.vector.tensor_copy, 0, WU_SPLIT), (nc.scalar.copy, WU_SPLIT, P)):
+            copy(
+                out=wu_grouped[:, :, m0:m1, :].rearrange("p d m j -> p m d j"),
+                in_=wu_raw[:, :, m0 * PACK:m1 * PACK].rearrange("p j (m d) -> p m d j", d=PACK),
+            )
+        wu_codes = keep.tile([P, K], U32, name="wu_codes", align_bytes=64)
+        wu_plane = keep.tile([P, K], U8, name="wu_plane", align_bytes=64)
+        nc.vector.quantize_mx(out=wu_codes[:].bitcast(FP8X4), scales=wu_plane[:], in_=wu_grouped[:].rearrange("p d m j -> p (d m j)"))
+
+        for (t0, width), raw in zip(TOKEN_CHUNKS, u_raw):
+            grouped = keep.tile([P, width, PACK], BF16, name="u_grouped%d" % t0, align_bytes=64)
+            share = width // 2 if t0 == 0 else width
+            for copy, c0, c1 in ((nc.vector.tensor_copy, 0, share), (nc.scalar.copy, share, width)):
+                if c1 > c0:
+                    copy(
+                        out=grouped[:, c0:c1, :].rearrange("p (c i) j -> p c j i", i=4),
+                        in_=raw[:, :, c0:c1].rearrange("p j (c i) -> p c j i", i=4),
+                    )
+            u_codes = keep.tile([P, width], U32, name="u_codes%d" % t0, align_bytes=64)
+            u_plane = keep.tile([P, width], U8, name="u_plane%d" % t0, align_bytes=64)
+            nc.vector.quantize_mx(out=u_codes[:].bitcast(FP8X4), scales=u_plane[:], in_=grouped[:].rearrange("p t j -> p (t j)"))
+            for u in range(2):
+                bank = psum.tile([P, BANK], F32, name="bank")
+                for e in range(2):
+                    d = 2 * u + e
+                    nc.tensor.matmul_mx(
+                        out=bank[:, e * width:(e + 1) * width],
+                        lhsT=wu_codes[:, d * P:(d + 1) * P].bitcast(FP8X4),
+                        lhsT_scale=wu_plane[:, d * P:(d + 1) * P],
+                        rhs=u_codes[:].bitcast(FP8X4),
+                        rhs_scale=u_plane[:],
+                        start=True,
+                        stop=True,
+                    )
+                copy = nc.vector.tensor_copy if (u == 0 and t0 + width == T) else nc.scalar.copy
+                copy(
+                    out=x_pairs[u][:, t0:t0 + width].bitcast(BF16).rearrange("p (t e) -> p t e", e=2),
+                    in_=bank[:, 0:2 * width].rearrange("p (e t) -> p t e", e=2),
+                )
+
+        x_codes = keep.tile([P, S], U32, name="x_codes", align_bytes=64)
+        x_plane = keep.tile([P, S], U8, name="x_plane", align_bytes=64)
+        y = [keep.tile([P, S], F32, name="y%d" % b) for b in range(N // P)]
+
+        def gather_slots(s0, width):
+            picked = ring.tile([P, 2, width], U32, name="picked")
+            for u in range(2):
+                nc.vector.tensor_copy(out=picked[:, u, :], in_=x_pairs[u][:].indirect(slot_tokens[:, s0 // PER_COL:(s0 + width) // PER_COL]))
+            return picked
+
+        def weave(width, picked):
+            woven = ring.tile([P, width, 2], U32, name="woven", align_bytes=64)
+            nc.scalar.copy(out=woven[:], in_=picked[:].rearrange("p u s -> p s u"))
+            return woven
+
+        def quantize_slots(s0, width, woven):
+            nc.vector.quantize_mx(
+                out=x_codes[:, s0:s0 + width].bitcast(FP8X4),
+                scales=x_plane[:, s0:s0 + width],
+                in_=woven[:].rearrange("p s u -> p (s u)").bitcast(BF16),
+            )
+
+        def multiply_slots(b, s0, width):
+            pool = late if b > 0 or s0 >= SLOT_CHUNKS[-2][0] else psum
+            bank = pool.tile([P, BANK], F32, name="bank")
+            for c0 in range(0, width, C):
+                e = (s0 + c0) // C
+                col = (e % EXPERTS_A_LOAD) * N + b * P
+                nc.tensor.matmul_mx(
+                    out=bank[:, c0:c0 + C],
+                    lhsT=w_codes[e // EXPERTS_A_LOAD][:, 2 * col:2 * (col + P)].bitcast(FP4X4),
+                    lhsT_scale=w_plane[:, e * N + b * P:e * N + (b + 1) * P],
+                    rhs=x_codes[:, s0 + c0:s0 + c0 + C].bitcast(FP8X4),
+                    rhs_scale=x_plane[:, s0 + c0:s0 + c0 + C],
+                    start=True,
+                    stop=True,
+                )
+            nc.scalar.copy(out=y[b][:, s0:s0 + width], in_=bank[:, 0:width])
+
+        waiting = None
+        for s0, width in SLOT_CHUNKS[:-1]:
+            picked = gather_slots(s0, width)
+            if waiting is not None:
+                quantize_slots(waiting[0], waiting[1], weave(waiting[1], waiting[2]))
+                multiply_slots(0, waiting[0], waiting[1])
+            waiting = (s0, width, picked)
+        s0, width = SLOT_CHUNKS[-1]
+        final = keep.tile([P, width, 2], U32, name="final", align_bytes=64)
+        for u in range(2):
+            nc.vector.tensor_copy(out=final[:, :, u], in_=x_pairs[u][:].indirect(slot_tokens[:, s0 // PER_COL:(s0 + width) // PER_COL]))
+        quantize_slots(waiting[0], waiting[1], weave(waiting[1], waiting[2]))
+        multiply_slots(0, waiting[0], waiting[1])
+        quantize_slots(s0, width, final)
+        multiply_slots(0, s0, width)
+        for b in (2, 1):
+            for s0 in range(0, S, BANK):
+                multiply_slots(b, s0, BANK)
+
+        def gated(b, r, t0, width):
+            product = prods.tile([P, width], F32, name="product")
+            nc.vector.tensor_tensor(
+                product[:], y[b][:].indirect(token_slots[r][:, t0 // PER_COL:(t0 + width) // PER_COL]), gates[:, r, t0:t0 + width], MULT
+            )
+            return product
+
+        def add_turned(bank, product, width, first, last):
+            for c0 in range(0, width, P):
+                nc.tensor.matmul(
+                    bank[:, c0:c0 + P], product[:, c0:c0 + P], ident[:], is_transpose=True,
+                    start=(first and c0 == 0), stop=(last and c0 == width - P),
+                )
+
+        def add_choice(b, r, turned, last):
+            product = gated(b, r, 0, T)
+            for bank, (t0, width) in zip(turned, HALVES):
+                add_turned(bank, product[:, t0:t0 + width], width, r == 0, last)
+
+        def turn_back(bank, t0, width):
+            staged = ring.tile([P, width], F32, name="staged%d" % t0)
+            nc.scalar.copy(out=staged[:], in_=bank[:, 0:width])
+            upright = psum.tile([P, BANK], F32, name="bank")
+            for c0 in range(0, width, P):
+                nc.tensor.transpose(upright[:, c0:c0 + P], staged[:, c0:c0 + P], ident[:])
+            return upright
+
+        def whole_block(b):
+            turned = [psum.tile([P, BANK], F32, name="bank") for h in HALVES]
+            for r in range(TOP):
+                add_choice(b, r, turned, r == TOP - 1)
+            for bank, (t0, width) in zip(turned, HALVES):
+                upright = turn_back(bank, t0, width)
+                result = ring.tile([P, width], F32, name="result%d" % t0)
+                nc.scalar.copy(out=result[:], in_=upright[:, 0:width])
+                nc.sync.dma_start(out=out[b * P:(b + 1) * P, t0:t0 + width], in_=result[:])
+
+        whole_block(0)
+        held = [psum.tile([P, BANK], F32, name="bank") for h in HALVES]
+        for r in range(TOP - 2):
+            add_choice(2, r, held, False)
+        whole_block(1)
+        partial = []
+        for bank, (t0, width) in zip(held, HALVES):
+            add_turned(bank, gated(2, TOP - 2, t0, width), width, False, True)
+            partial.append(turn_back(bank, t0, width))
+        last = [gated(2, TOP - 1, t0, width) for t0, width in HALVES]
+        for product, bank, (t0, width) in zip(last, partial, HALVES):
+            result = ring.tile([P, width], F32, name="result%d" % t0)
+            nc.vector.tensor_tensor(result[:], bank[:, 0:width], product[:], ADD)
+            nc.sync.dma_start(out=out[2 * P:3 * P, t0:t0 + width], in_=result[:])

@@ -28,7 +28,7 @@ WINDOW = 704
 TOKEN_CHUNKS = ((0, 256), (256, 256), (512, 128))
 SLOT_CHUNKS = ((0, 512), (512, 512), (1024, 512), (1536, 512), (2048, 256), (2304, 128), (2432, 128))
 EXPERTS_A_LOAD = 4
-WU_SPLIT = 88
+WU_SPLIT = 44
 HALVES = ((0, 384), (384, 256))
 
 
@@ -38,14 +38,17 @@ def tile_moe_prv_lin_none_kernel(tc, uT, wu, w_words, w_scales, gate, offs, pos1
         lists = ctx.enter_context(tc.tile_pool(name="lists", bufs=1))
         keep = ctx.enter_context(tc.tile_pool(name="keep", bufs=1))
         ring = ctx.enter_context(tc.tile_pool(name="ring", bufs=2))
-        prods = ctx.enter_context(tc.tile_pool(name="prods", bufs=6))
+        prods = ctx.enter_context(tc.tile_pool(name="prods", bufs=14))
         psum = ctx.enter_context(tc.psum_pool(name="psum", bufs=6))
         late = ctx.enter_context(tc.psum_pool(name="late", bufs=2))
 
         wu_rows = wu.rearrange("(p j) k -> p j k", j=PACK)
         u_rows = uT.rearrange("(p j) t -> p j t", j=PACK)
-        wu_raw = keep.tile([P, PACK, K], F32, name="wu_raw")
-        nc.sync.dma_start(out=wu_raw[:], in_=wu_rows)
+        wu_raw = []
+        for h in range(2):
+            raw = keep.tile([P, PACK, K // 2], F32, name="wu_raw%d" % h)
+            nc.sync.dma_start(out=raw[:], in_=wu_rows[:, :, h * (K // 2):(h + 1) * (K // 2)])
+            wu_raw.append(raw)
         u_raw = []
         for t0, width in TOKEN_CHUNKS:
             raw = keep.tile([P, PACK, width], F32, name="u_raw%d" % t0)
@@ -87,11 +90,13 @@ def tile_moe_prv_lin_none_kernel(tc, uT, wu, w_words, w_scales, gate, offs, pos1
             x_pairs.append(pair)
 
         wu_grouped = keep.tile([P, PACK, P, PACK], BF16, name="wu_grouped", align_bytes=64)
-        for copy, m0, m1 in ((nc.vector.tensor_copy, 0, WU_SPLIT), (nc.scalar.copy, WU_SPLIT, P)):
-            copy(
-                out=wu_grouped[:, :, m0:m1, :].rearrange("p d m j -> p m d j"),
-                in_=wu_raw[:, :, m0 * PACK:m1 * PACK].rearrange("p j (m d) -> p m d j", d=PACK),
-            )
+        half = P // 2
+        for h in range(2):
+            for copy, m0, m1 in ((nc.vector.tensor_copy, 0, WU_SPLIT), (nc.scalar.copy, WU_SPLIT, half)):
+                copy(
+                    out=wu_grouped[:, :, h * half + m0:h * half + m1, :],
+                    in_=wu_raw[h][:, :, m0 * PACK:m1 * PACK].rearrange("p j (m d) -> p d m j", d=PACK),
+                )
         wu_codes = keep.tile([P, K], U32, name="wu_codes", align_bytes=64)
         wu_plane = keep.tile([P, K], U8, name="wu_plane", align_bytes=64)
         nc.vector.quantize_mx(out=wu_codes[:].bitcast(FP8X4), scales=wu_plane[:], in_=wu_grouped[:].rearrange("p d m j -> p (d m j)"))
@@ -102,8 +107,8 @@ def tile_moe_prv_lin_none_kernel(tc, uT, wu, w_words, w_scales, gate, offs, pos1
             for copy, c0, c1 in ((nc.vector.tensor_copy, 0, share), (nc.scalar.copy, share, width)):
                 if c1 > c0:
                     copy(
-                        out=grouped[:, c0:c1, :].rearrange("p (c i) j -> p c j i", i=4),
-                        in_=raw[:, :, c0:c1].rearrange("p j (c i) -> p c j i", i=4),
+                        out=grouped[:, c0:c1, :],
+                        in_=raw[:, :, c0:c1].rearrange("p j t -> p t j"),
                     )
             u_codes = keep.tile([P, width], U32, name="u_codes%d" % t0, align_bytes=64)
             u_plane = keep.tile([P, width], U8, name="u_plane%d" % t0, align_bytes=64)
@@ -181,7 +186,7 @@ def tile_moe_prv_lin_none_kernel(tc, uT, wu, w_words, w_scales, gate, offs, pos1
         multiply_slots(0, waiting[0], waiting[1])
         quantize_slots(s0, width, final)
         multiply_slots(0, s0, width)
-        for b in (2, 1):
+        for b in (1, 2):
             for s0 in range(0, S, BANK):
                 multiply_slots(b, s0, BANK)
 
@@ -223,10 +228,10 @@ def tile_moe_prv_lin_none_kernel(tc, uT, wu, w_words, w_scales, gate, offs, pos1
                 nc.sync.dma_start(out=out[b * P:(b + 1) * P, t0:t0 + width], in_=result[:])
 
         whole_block(0)
+        whole_block(1)
         held = [psum.tile([P, BANK], F32, name="bank") for h in HALVES]
         for r in range(TOP - 2):
             add_choice(2, r, held, False)
-        whole_block(1)
         partial = []
         for bank, (t0, width) in zip(held, HALVES):
             add_turned(bank, gated(2, TOP - 2, t0, width), width, False, True)

@@ -137,7 +137,7 @@ def tile_moe_prv_lin_none_kernel(tc, uT, wu, w_words, w_scales, gate, offs, pos1
         y = [keep.tile([P, S], F32, name="y%d" % b) for b in range(N // P)]
 
         def gather_slots(s0, width):
-            picked = ring.tile([P, 2, width], U32, name="picked")
+            picked = ring.tile([P, 2, width], U32, name="picked", align_bytes=64)
             for u in range(2):
                 nc.vector.tensor_copy(out=picked[:, u, :], in_=x_pairs[u][:].indirect(slot_tokens[:, s0 // PER_COL:(s0 + width) // PER_COL]))
             return picked
@@ -169,7 +169,8 @@ def tile_moe_prv_lin_none_kernel(tc, uT, wu, w_words, w_scales, gate, offs, pos1
                     start=True,
                     stop=True,
                 )
-            nc.scalar.copy(out=y[b][:, s0:s0 + width], in_=bank[:, 0:width])
+            copy = nc.vector.tensor_copy if (b == 0 and s0 + width == S) else nc.scalar.copy
+            copy(out=y[b][:, s0:s0 + width], in_=bank[:, 0:width])
 
         waiting = None
         for s0, width in SLOT_CHUNKS[:-1]:
@@ -179,7 +180,7 @@ def tile_moe_prv_lin_none_kernel(tc, uT, wu, w_words, w_scales, gate, offs, pos1
                 multiply_slots(0, waiting[0], waiting[1])
             waiting = (s0, width, picked)
         s0, width = SLOT_CHUNKS[-1]
-        final = keep.tile([P, width, 2], U32, name="final", align_bytes=64)
+        final = ring.tile([P, width, 2], U32, name="picked", align_bytes=64)
         for u in range(2):
             nc.vector.tensor_copy(out=final[:, :, u], in_=x_pairs[u][:].indirect(slot_tokens[:, s0 // PER_COL:(s0 + width) // PER_COL]))
         quantize_slots(waiting[0], waiting[1], weave(waiting[1], waiting[2]))

@@ -144,7 +144,10 @@ def tile_moe_prv_lin_none_kernel(tc, uT, wu, w_words, w_scales, gate, offs, pos1
 
         def weave(width, picked):
             woven = ring.tile([P, width, 2], U32, name="woven", align_bytes=64)
-            nc.scalar.copy(out=woven[:], in_=picked[:].rearrange("p u s -> p s u"))
+            if width == C:
+                nc.vector.tensor_copy(out=woven[:].bitcast(I32), in_=picked[:].bitcast(I32).rearrange("p u s -> p s u"))
+            else:
+                nc.scalar.copy(out=woven[:], in_=picked[:].rearrange("p u s -> p s u"))
             return woven
 
         def quantize_slots(s0, width, woven):

from contextlib import ExitStack

import concourse.mybir as mybir
from concourse.masks import make_identity

M, K, N, T = 512, 512, 384, 640
E, C, TOP = 20, 128, 4
S = E * C

FLOPS = 2 * M * K * T + 2 * K * N * S

F32 = mybir.dt.float32
BF16 = mybir.dt.bfloat16
I32 = mybir.dt.int32
U32 = mybir.dt.uint32
U16 = mybir.dt.uint16
U8 = mybir.dt.uint8
FP8X4 = mybir.dt.float8_e4m3fn_x4
FP4X4 = mybir.dt.float4_e2m1fn_x4
MULT = mybir.AluOpType.mult
ADD = mybir.AluOpType.add

P = 128
PACK = 4
BANK = 512
PER_COL = 16
WINDOW = 704
TOKEN_CHUNKS = ((0, 256), (256, 256), (512, 128))
SLOT_CHUNKS = ((0, 512), (512, 512), (1024, 512), (1536, 512), (2048, 256), (2304, 128), (2432, 128))
EXPERTS_A_LOAD = 4
WU_SPLIT = 44
HALVES = ((0, 384), (384, 256))


def tile_moe_prv_lin_none_kernel(tc, uT, wu, w_words, w_scales, gate, offs, pos1, pos2, pos3, pos4, out):
    nc = tc.nc
    with ExitStack() as ctx:
        lists = ctx.enter_context(tc.tile_pool(name="lists", bufs=1))
        keep = ctx.enter_context(tc.tile_pool(name="keep", bufs=1))
        ring = ctx.enter_context(tc.tile_pool(name="ring", bufs=2))
        prods = ctx.enter_context(tc.tile_pool(name="prods", bufs=14))
        psum = ctx.enter_context(tc.psum_pool(name="psum", bufs=6))
        late = ctx.enter_context(tc.psum_pool(name="late", bufs=2))

        wu_rows = wu.rearrange("(p j) k -> p j k", j=PACK)
        u_rows = uT.rearrange("(p j) t -> p j t", j=PACK)
        wu_raw = []
        for h in range(2):
            raw = keep.tile([P, PACK, K // 2], F32, name="wu_raw%d" % h)
            nc.sync.dma_start(out=raw[:], in_=wu_rows[:, :, h * (K // 2):(h + 1) * (K // 2)])
            wu_raw.append(raw)
        u_raw = []
        for t0, width in TOKEN_CHUNKS:
            raw = keep.tile([P, PACK, width], F32, name="u_raw%d" % t0)
            nc.sync.dma_start(out=raw[:], in_=u_rows[:, :, t0:t0 + width])
            u_raw.append(raw)
        slot_tokens = lists.tile([P, S // PER_COL], U16, name="slot_tokens")
        nc.sync.dma_start(slot_tokens[:], offs)

        w_plane = keep.tile([P, E * N], U8, name="w_plane", align_bytes=64)
        nc.vector.memset(w_plane[:].bitcast(I32), 0)
        for r in range(4):
            nc.sync.dma_start(
                out=w_plane[r:P:32, :].bitcast(I32).rearrange("q (e n) -> q e n", e=E),
                in_=w_scales[:, 0, r:16:4, :].bitcast(I32).rearrange("e q n -> q e n"),
            )
        w_codes = []
        for g in range(E // EXPERTS_A_LOAD):
            codes = keep.tile([P, EXPERTS_A_LOAD * 2 * N], U8, name="w_codes%d" % g, align_bytes=64)
            nc.sync.dma_start(
                out=codes[:].bitcast(I32).rearrange("p (e n) -> p e n", e=EXPERTS_A_LOAD),
                in_=w_words[g * EXPERTS_A_LOAD:(g + 1) * EXPERTS_A_LOAD, 0, :, :].bitcast(I32).rearrange("e p n -> p e n"),
            )
            w_codes.append(codes)
        token_slots = []
        for r, pos in enumerate((pos1, pos2, pos3, pos4)):
            one = lists.tile([P, T // PER_COL], U16, name="token_slots%d" % r)
            nc.sync.dma_start(one[:], pos)
            token_slots.append(one)
        gates = keep.tile([P, TOP, T], F32, name="gates")
        nc.sync.dma_start(out=gates[:], in_=gate[:, 0:P, :].rearrange("r p t -> p r t"))

        ident = keep.tile([P, P], F32, name="ident")
        make_identity(nc, ident[:])

        x_pairs = []
        for u in range(2):
            pair = keep.tile([P, WINDOW], U32, name="x_pairs%d" % u)
            nc.vector.memset(pair[:, T:WINDOW], 0)
            x_pairs.append(pair)

        wu_grouped = keep.tile([P, PACK, P, PACK], BF16, name="wu_grouped", align_bytes=64)
        half = P // 2
        for h in range(2):
            for copy, m0, m1 in ((nc.vector.tensor_copy, 0, WU_SPLIT), (nc.scalar.copy, WU_SPLIT, half)):
                copy(
                    out=wu_grouped[:, :, h * half + m0:h * half + m1, :],
                    in_=wu_raw[h][:, :, m0 * PACK:m1 * PACK].rearrange("p j (m d) -> p d m j", d=PACK),
                )
        wu_codes = keep.tile([P, K], U32, name="wu_codes", align_bytes=64)
        wu_plane = keep.tile([P, K], U8, name="wu_plane", align_bytes=64)
        nc.vector.quantize_mx(out=wu_codes[:].bitcast(FP8X4), scales=wu_plane[:], in_=wu_grouped[:].rearrange("p d m j -> p (d m j)"))

        for (t0, width), raw in zip(TOKEN_CHUNKS, u_raw):
            grouped = keep.tile([P, width, PACK], BF16, name="u_grouped%d" % t0, align_bytes=64)
            share = width // 2 if t0 == 0 else width
            for copy, c0, c1 in ((nc.vector.tensor_copy, 0, share), (nc.scalar.copy, share, width)):
                if c1 > c0:
                    copy(
                        out=grouped[:, c0:c1, :],
                        in_=raw[:, :, c0:c1].rearrange("p j t -> p t j"),
                    )
            u_codes = keep.tile([P, width], U32, name="u_codes%d" % t0, align_bytes=64)
            u_plane = keep.tile([P, width], U8, name="u_plane%d" % t0, align_bytes=64)
            nc.vector.quantize_mx(out=u_codes[:].bitcast(FP8X4), scales=u_plane[:], in_=grouped[:].rearrange("p t j -> p (t j)"))
            for u in range(2):
                bank = psum.tile([P, BANK], F32, name="bank")
                for e in range(2):
                    d = 2 * u + e
                    nc.tensor.matmul_mx(
                        out=bank[:, e * width:(e + 1) * width],
                        lhsT=wu_codes[:, d * P:(d + 1) * P].bitcast(FP8X4),
                        lhsT_scale=wu_plane[:, d * P:(d + 1) * P],
                        rhs=u_codes[:].bitcast(FP8X4),
                        rhs_scale=u_plane[:],
                        start=True,
                        stop=True,
                    )
                copy = nc.vector.tensor_copy if (u == 0 and t0 + width == T) else nc.scalar.copy
                copy(
                    out=x_pairs[u][:, t0:t0 + width].bitcast(BF16).rearrange("p (t e) -> p t e", e=2),
                    in_=bank[:, 0:2 * width].rearrange("p (e t) -> p t e", e=2),
                )

        x_codes = keep.tile([P, S], U32, name="x_codes", align_bytes=64)
        x_plane = keep.tile([P, S], U8, name="x_plane", align_bytes=64)
        y = [keep.tile([P, S], F32, name="y%d" % b) for b in range(N // P)]

        def gather_slots(s0, width):
            picked = ring.tile([P, 2, width], U32, name="picked", align_bytes=64)
            for u in range(2):
                nc.vector.tensor_copy(out=picked[:, u, :], in_=x_pairs[u][:].indirect(slot_tokens[:, s0 // PER_COL:(s0 + width) // PER_COL]))
            return picked

        def weave(width, picked):
            woven = ring.tile([P, width, 2], U32, name="woven", align_bytes=64)
            if width == C:
                nc.vector.tensor_copy(out=woven[:].bitcast(I32), in_=picked[:].bitcast(I32).rearrange("p u s -> p s u"))
            else:
                nc.scalar.copy(out=woven[:], in_=picked[:].rearrange("p u s -> p s u"))
            return woven

        def quantize_slots(s0, width, woven):
            nc.vector.quantize_mx(
                out=x_codes[:, s0:s0 + width].bitcast(FP8X4),
                scales=x_plane[:, s0:s0 + width],
                in_=woven[:].rearrange("p s u -> p (s u)").bitcast(BF16),
            )

        def multiply_slots(b, s0, width):
            pool = late if b > 0 or s0 >= SLOT_CHUNKS[-2][0] else psum
            bank = pool.tile([P, BANK], F32, name="bank")
            for c0 in range(0, width, C):
                e = (s0 + c0) // C
                col = (e % EXPERTS_A_LOAD) * N + b * P
                nc.tensor.matmul_mx(
                    out=bank[:, c0:c0 + C],
                    lhsT=w_codes[e // EXPERTS_A_LOAD][:, 2 * col:2 * (col + P)].bitcast(FP4X4),
                    lhsT_scale=w_plane[:, e * N + b * P:e * N + (b + 1) * P],
                    rhs=x_codes[:, s0 + c0:s0 + c0 + C].bitcast(FP8X4),
                    rhs_scale=x_plane[:, s0 + c0:s0 + c0 + C],
                    start=True,
                    stop=True,
                )
            copy = nc.vector.tensor_copy if (b == 0 and s0 + width == S) else nc.scalar.copy
            copy(out=y[b][:, s0:s0 + width], in_=bank[:, 0:width])

        waiting = None
        for s0, width in SLOT_CHUNKS[:-1]:
            picked = gather_slots(s0, width)
            if waiting is not None:
                quantize_slots(waiting[0], waiting[1], weave(waiting[1], waiting[2]))
                multiply_slots(0, waiting[0], waiting[1])
            waiting = (s0, width, picked)
        s0, width = SLOT_CHUNKS[-1]
        final = ring.tile([P, width, 2], U32, name="picked", align_bytes=64)
        for u in range(2):
            nc.vector.tensor_copy(out=final[:, :, u], in_=x_pairs[u][:].indirect(slot_tokens[:, s0 // PER_COL:(s0 + width) // PER_COL]))
        quantize_slots(waiting[0], waiting[1], weave(waiting[1], waiting[2]))
        multiply_slots(0, waiting[0], waiting[1])
        quantize_slots(s0, width, final)
        multiply_slots(0, s0, width)
        for b in (1, 2):
            for s0 in range(0, S, BANK):
                multiply_slots(b, s0, BANK)

        def gated(b, r, t0, width):
            product = prods.tile([P, width], F32, name="product")
            nc.vector.tensor_tensor(
                product[:], y[b][:].indirect(token_slots[r][:, t0 // PER_COL:(t0 + width) // PER_COL]), gates[:, r, t0:t0 + width], MULT
            )
            return product

        def add_turned(bank, product, width, first, last):
            for c0 in range(0, width, P):
                nc.tensor.matmul(
                    bank[:, c0:c0 + P], product[:, c0:c0 + P], ident[:], is_transpose=True,
                    start=(first and c0 == 0), stop=(last and c0 == width - P),
                )

        def add_choice(b, r, turned, last):
            product = gated(b, r, 0, T)
            for bank, (t0, width) in zip(turned, HALVES):
                add_turned(bank, product[:, t0:t0 + width], width, r == 0, last)

        def turn_back(bank, t0, width):
            staged = ring.tile([P, width], F32, name="staged%d" % t0)
            nc.scalar.copy(out=staged[:], in_=bank[:, 0:width])
            upright = psum.tile([P, BANK], F32, name="bank")
            for c0 in range(0, width, P):
                nc.tensor.transpose(upright[:, c0:c0 + P], staged[:, c0:c0 + P], ident[:])
            return upright

        def whole_block(b):
            turned = [psum.tile([P, BANK], F32, name="bank") for h in HALVES]
            for r in range(TOP):
                add_choice(b, r, turned, r == TOP - 1)
            for bank, (t0, width) in zip(turned, HALVES):
                upright = turn_back(bank, t0, width)
                result = ring.tile([P, width], F32, name="result%d" % t0)
                nc.scalar.copy(out=result[:], in_=upright[:, 0:width])
                nc.sync.dma_start(out=out[b * P:(b + 1) * P, t0:t0 + width], in_=result[:])

        whole_block(0)
        whole_block(1)
        held = [psum.tile([P, BANK], F32, name="bank") for h in HALVES]
        for r in range(TOP - 2):
            add_choice(2, r, held, False)
        partial = []
        for bank, (t0, width) in zip(held, HALVES):
            add_turned(bank, gated(2, TOP - 2, t0, width), width, False, True)
            partial.append(turn_back(bank, t0, width))
        last = [gated(2, TOP - 1, t0, width) for t0, width in HALVES]
        for product, bank, (t0, width) in zip(last, partial, HALVES):
            result = ring.tile([P, width], F32, name="result%d" % t0)
            nc.vector.tensor_tensor(result[:], bank[:, 0:width], product[:], ADD)
            nc.sync.dma_start(out=out[2 * P:3 * P, t0:t0 + width], in_=result[:])
